import numpy as np
import ml_dtypes


def mxq(x, axis, fmt="e4m3"):
    dtype, down = {"e4m3": (ml_dtypes.float8_e4m3fn, 7), "e5m2": (ml_dtypes.float8_e5m2, 14)}[fmt]
    v = np.moveaxis(np.asarray(x, np.float32).astype(ml_dtypes.bfloat16).astype(np.float64), axis, -1)
    blocks = v.reshape(v.shape[:-1] + (-1, 32))
    amax = np.abs(blocks).max(-1, keepdims=True)
    byte = np.maximum(np.where(amax > 0, np.frexp(amax)[1] - 1 + 127, 0) - down, 1)
    scale = np.exp2(byte - 127.0)
    codes = (blocks / scale).astype(np.float32).astype(dtype).astype(np.float64)
    return np.moveaxis((codes * scale).reshape(v.shape), -1, axis)


WIDE = False


def mx_kscale(k):
    if not WIDE:
        return np.ones(k)
    levels = np.array([10, -10, 5, -5, 0])
    if k % 512:
        return np.exp2(np.random.permutation(np.resize(levels, k // 32))).repeat(32)
    a = np.empty((k // 512, 16))
    for p in range(k // 512):
        a[p, :8] = np.random.permutation(np.resize(levels, 8))
        for g in range(8):
            far = levels[np.abs(levels - a[p, g]) >= 10]
            a[p, g + 8] = far[np.random.randint(len(far))]
    return np.exp2(a.ravel()).repeat(32)


def f64(x):
    return np.asarray(x).astype(np.float64)


def striped(idx):
    return np.tile(idx.reshape(-1, 16).T, (8, 1)).astype(np.uint16)


def unstriped(offs):
    return offs[:16].T.reshape(-1).astype(np.int64)


def striped8(idx):
    return np.concatenate([x.reshape(-1, 16).T for x in idx]).astype(np.uint16)


def runs(offs, k):
    lists = np.stack([offs[16 * r : 16 * r + 16].T.reshape(-1) for r in range(8)]).astype(np.int64)
    return lists[np.arange(k) % 512 // 64]


def pack_weight(w):
    k, n = w.shape
    w = f64(np.asarray(w, np.float32).astype(ml_dtypes.bfloat16)).reshape(k // 32, 32, n)
    amax = np.abs(w).max(1)
    byte = np.clip(np.where(amax > 0, np.frexp(amax)[1] - 1 + 127 - 7, 1), 1, 254)
    scaled = (w * np.exp2(127.0 - byte)[:, None, :]).reshape(k, n).astype(np.float32)
    words = np.ascontiguousarray(scaled.reshape(k // 512, 128, 4, n).transpose(0, 1, 3, 2)).astype(ml_dtypes.float8_e4m3fn).view(np.uint8)
    return words, np.ascontiguousarray(byte.astype(np.uint8).reshape(k // 512, 16, n))


def unpack_weight(words, scales):
    g, p, n, _ = words.shape
    vals = np.ascontiguousarray(words).view(ml_dtypes.float8_e4m3fn).astype(np.float64) * np.repeat(np.exp2(scales.astype(np.float64) - 127.0), 8, axis=1)[..., None]
    return vals.transpose(0, 1, 3, 2).reshape(g * 512, n)


E2M1 = np.array([0.0, 0.5, 1.0, 1.5, 2.0, 3.0, 4.0, 6.0, -0.0, -0.5, -1.0, -1.5, -2.0, -3.0, -4.0, -6.0])


def pack_fp4(w):
    k, n = w.shape
    w = f64(np.asarray(w, np.float32).astype(ml_dtypes.bfloat16)).reshape(k // 32, 32, n)
    amax = np.abs(w).max(1)
    mant, ex = np.frexp(amax / 6.0)
    byte = np.clip(np.where(amax > 0, np.where(mant > 0.5, ex, ex - 1) + 127, 1), 1, 254)
    scaled = (w * np.exp2(127.0 - byte)[:, None, :]).reshape(k, n).astype(np.float32)
    c = np.ascontiguousarray(scaled.reshape(k // 512, 128, 4, n).transpose(0, 1, 3, 2)).astype(ml_dtypes.float4_e2m1fn).view(np.uint8) & 0xF
    words = (c[..., 0::2] | (c[..., 1::2] << 4)).reshape(k // 512, 128, 2 * n)
    return np.ascontiguousarray(words), np.ascontiguousarray(byte.astype(np.uint8).reshape(k // 512, 16, n))


def unpack_fp4(words, scales):
    g, _, n = scales.shape
    words = np.ascontiguousarray(words).reshape(g, 128, n, 2)
    nib = np.empty((g, 128, n, 4), np.uint8)
    nib[..., 0::2] = words & 0xF
    nib[..., 1::2] = words >> 4
    vals = E2M1[nib] * np.repeat(np.exp2(scales.astype(np.float64) - 127.0), 8, axis=1)[..., None]
    return vals.transpose(0, 1, 3, 2).reshape(g * 512, n)


def sigmoid(v):
    return 1.0 / (1.0 + np.exp(-np.maximum(v, -700.0)))

def planes(y):
    n, m = y.shape
    v = y.astype(np.float32).astype(ml_dtypes.bfloat16).astype(np.float64).reshape(n // 32, 32, m)
    top = np.abs(v).max(1)
    byte = np.clip(np.where(top > 0, np.frexp(top)[1] - 1 + 127 - 7, 1), 1, 254)
    codes = (v * np.exp2(127.0 - byte)[:, None, :]).reshape(n, m).astype(np.float32).astype(ml_dtypes.float8_e4m3fn).view(np.uint8)
    words = codes.reshape(n // 512, 128, 4, m).transpose(0, 1, 3, 2)
    return np.ascontiguousarray(words), np.ascontiguousarray(byte.astype(np.uint8).reshape(n // 512, 16, m))


K, T, S, N, H = 512, 2048, 512, 512, 512


def setup_inputs():
    n = np.random.standard_normal
    s = mx_kscale(K)[:, None]
    u = mx_kscale(H)
    packed_xT = pack_weight(n((K, T)) * s)
    packed_w1 = pack_fp4(n((K, H)) / np.sqrt(K) / s)
    packed_w2 = pack_fp4(n((K, H)) / np.sqrt(K) / s)
    packed_w3 = pack_fp4(n((H, N)) / np.sqrt(H) / u[:, None])
    return {
        "x_words": packed_xT[0],
        "x_scales": packed_xT[1],
        "w1_words": packed_w1[0],
        "w1_scales": packed_w1[1],
        "w2_words": packed_w2[0],
        "w2_scales": packed_w2[1],
        "gn": (np.random.uniform(0.5, 1.5, (H, 1)) * u[:, None]).astype(np.float32),
        "w3_words": packed_w3[0],
        "w3_scales": packed_w3[1],
        "offs": striped(np.random.permutation(T)[:S]),
        "two": striped(np.random.permutation(T)[:S]),
        "n1": striped8(np.stack([np.random.permutation(S) for _ in range(8)])),
        "n2": striped8(np.stack([np.random.permutation(S) for _ in range(8)])),
        "n3": striped8(np.stack([np.random.permutation(S) for _ in range(8)])),
        "n4": striped8(np.stack([np.random.permutation(S) for _ in range(8)])),
    }


def reference(x_words, x_scales, w1_words, w1_scales, w2_words, w2_scales, gn, w3_words, w3_scales, offs, two, n1, n2, n3, n4):
    xq = unpack_weight(x_words, x_scales)[:, unstriped(offs)]
    y = unpack_fp4(w1_words, w1_scales).T @ xq
    x_two = unpack_weight(x_words, x_scales)[:, unstriped(two)]
    d = unpack_fp4(w2_words, w2_scales).T @ x_two
    z = f64(gn) * (0.75 * (y * (d[np.arange(H)[:, None], runs(n2, H)]) - ((y[np.arange(H)[:, None], runs(n1, H)]) * d)))
    h = unpack_fp4(w3_words, w3_scales).T @ mxq(z, 0, "e4m3")
    out_0 = h * (sigmoid(h[np.arange(N)[:, None], runs(n3, N)] - (h[np.arange(N)[:, None], runs(n4, N)])))
    return (out_0,) + planes(out_0)

@@ -1,0 +1,215 @@
+from contextlib import ExitStack
+
+import concourse.mybir as mybir
+
+K, T, S, N, H = 512, 2048, 512, 512, 512
+FLOPS = 3 * 2 * 512 * 512 * 512
+
+F32 = mybir.dt.float32
+BF16 = mybir.dt.bfloat16
+I32 = mybir.dt.int32
+U32 = mybir.dt.uint32
+U16 = mybir.dt.uint16
+U8 = mybir.dt.uint8
+FP8X4 = mybir.dt.float8_e4m3fn_x4
+FP4X4 = mybir.dt.float4_e2m1fn_x4
+ALU = mybir.AluOpType
+ACT = mybir.ActivationFunctionType
+
+P = 128
+PACK = 4
+QUADS = 4
+LIST_ROWS = 16
+PIECE = 128
+Z_CHUNKS = ((0, 256), (256, 128), (384, 128))
+OUT_CHUNKS = ((0, 256), (256, 128), (384, 128))
+
+
+def entries(lst, first, count):
+    return lst[:, first // LIST_ROWS : (first + count) // LIST_ROWS]
+
+
+def load_scale_rows(queue, plane, scales):
+    rows = scales[0].bitcast(I32).rearrange("(q r) c -> r q c", r=4)
+    for r in range(4):
+        queue.dma_start(out=plane[r:P:32, :].bitcast(I32), in_=rows[r])
+
+
+def deal_words(engine, words, dealt):
+    engine.tensor_copy(
+        out=dealt[:].rearrange("p t (m e) -> p t m e", e=2),
+        in_=words[:].rearrange("p (m t e) -> p t m e", t=PACK, e=2),
+    )
+
+
+def deal_plane(engine, plane, dealt):
+    engine.tensor_copy(out=dealt[:], in_=plane[:].rearrange("p (m t) -> p t m", t=PACK))
+
+
+def by_words(tile_pt):
+    return tile_pt.rearrange("p t (c i) -> p c t i", i=4)
+
+
+def as_words(tile_words):
+    return tile_words.rearrange("p (c i) t -> p c t i", i=4)
+
+
+def tile_picked_twlcrossbcmp_none_po_kernel(
+    tc, x_words, x_scales, w1_words, w1_scales, w2_words, w2_scales, gn, w3_words, w3_scales,
+    offs, two, n1, n2, n3, n4, out_0, out_1, out_2,
+):
+    nc = tc.nc
+    with ExitStack() as ctx:
+        lists = ctx.enter_context(tc.tile_pool(name="lists", bufs=1))
+        keep = ctx.enter_context(tc.tile_pool(name="keep", bufs=1))
+        psum = ctx.enter_context(tc.psum_pool(name="psum", bufs=1))
+
+        def sb(name, shape, dtype):
+            return keep.tile(shape, dtype, name=name, align_bytes=64)
+
+        list_tiles = {}
+        for name in ("offs", "two", "n1", "n2", "n3", "n4"):
+            list_tiles[name] = lists.tile([P, S // LIST_ROWS], U16, name=name)
+
+        x_plane = sb("x_plane", [P, T], U8)
+        x_codes = sb("x_codes", [P, T], U32)
+        w_words = [sb("w_words%d" % i, [P, 2 * H], U8) for i in range(3)]
+        w_plane = [sb("w_plane%d" % i, [P, H], U8) for i in range(3)]
+        wd_words = [sb("wd_words%d" % i, [P, PACK, 2 * P], U8) for i in range(3)]
+        wd_plane = [sb("wd_plane%d" % i, [P, PACK, P], U8) for i in range(3)]
+        gain = sb("gain", [P, PACK], F32)
+        warm = sb("warm", [P, 2], F32)
+
+        nc.vector.memset(x_plane[:].bitcast(I32), 0)
+        for i in range(3):
+            nc.gpsimd.memset(w_plane[i][:].bitcast(I32), 0)
+        nc.vector.memset(warm[:, 0:1], 0.0)
+        nc.scalar.activation(warm[:, 1:2], warm[:, 0:1], ACT.Sigmoid)
+
+        load_scale_rows(nc.sync, x_plane, x_scales)
+        nc.sync.dma_start(list_tiles["offs"][:], offs)
+        nc.sync.dma_start(list_tiles["two"][:], two)
+        nc.sync.dma_start(out=w_words[0][:].bitcast(I32), in_=w1_words[0].bitcast(I32))
+        nc.sync.dma_start(out=w_words[1][:].bitcast(I32), in_=w2_words[0].bitcast(I32))
+        nc.sync.dma_start(out=x_codes[:].bitcast(I32), in_=x_words[0].rearrange("p n t -> p (n t)").bitcast(I32))
+        load_scale_rows(nc.sync, w_plane[0], w1_scales)
+        load_scale_rows(nc.sync, w_plane[1], w2_scales)
+        nc.sync.dma_start(out=gain[:], in_=gn.rearrange("(p t) o -> p (t o)", t=PACK))
+        nc.sync.dma_start(list_tiles["n2"][:], n2)
+        nc.sync.dma_start(list_tiles["n1"][:], n1)
+        nc.sync.dma_start(out=w_words[2][:].bitcast(I32), in_=w3_words[0].bitcast(I32))
+        load_scale_rows(nc.sync, w_plane[2], w3_scales)
+        nc.sync.dma_start(list_tiles["n4"][:], n4)
+        nc.sync.dma_start(list_tiles["n3"][:], n3)
+
+        a_codes = sb("a_codes", [P, S], U32)
+        a_plane = sb("a_plane", [P, S], U8)
+        b_codes = sb("b_codes", [P, S], U32)
+        b_plane = sb("b_plane", [P, S], U8)
+        nc.vector.tensor_copy(a_plane[:], x_plane[:].indirect(list_tiles["offs"][:]))
+        nc.vector.tensor_copy(b_plane[:], x_plane[:].indirect(list_tiles["two"][:]))
+        deal_words(nc.vector, w_words[0], wd_words[0])
+        deal_words(nc.vector, w_words[1], wd_words[1])
+        deal_plane(nc.vector, w_plane[0], wd_plane[0])
+        nc.vector.tensor_copy(a_codes[:], x_codes[:].indirect(list_tiles["offs"][:]))
+        deal_plane(nc.vector, w_plane[1], wd_plane[1])
+        half = S // 2
+        for first in (0, half):
+            nc.vector.tensor_copy(
+                b_codes[:, first : first + half], x_codes[:].indirect(entries(list_tiles["two"], first, half))
+            )
+        deal_words(nc.vector, w_words[2], wd_words[2])
+        deal_plane(nc.vector, w_plane[2], wd_plane[2])
+
+        def product(acc, w, t, codes, plane):
+            nc.tensor.matmul_mx(
+                out=acc, lhsT=wd_words[w][:, t, :].bitcast(FP4X4), lhsT_scale=wd_plane[w][:, t, :],
+                rhs=codes.bitcast(FP8X4), rhs_scale=plane, start=True, stop=True,
+            )
+
+        y = [sb("y%d" % t, [P, S], F32) for t in range(PACK)]
+        d = [sb("d%d" % t, [P, S], F32) for t in range(PACK)]
+        y_acc = [psum.tile([P, S], F32, name="bank%d" % t) for t in range(PACK)]
+        d_acc = [psum.tile([P, S], F32, name="bank%d" % (PACK + t)) for t in range(PACK)]
+        for t in range(PACK):
+            product(y_acc[t][:], 0, t, a_codes[:], a_plane[:])
+        for first in (0, half):
+            cols = slice(first, first + half)
+            product(d_acc[0][:, cols], 1, 0, b_codes[:, cols], b_plane[:, cols])
+        for t in range(1, PACK):
+            product(d_acc[t][:], 1, t, b_codes[:], b_plane[:])
+        for t in range(PACK):
+            nc.scalar.activation(y[t][:], y_acc[t][:], ACT.Copy, scale=gain[:, t : t + 1])
+            nc.scalar.activation(d[t][:], d_acc[t][:], ACT.Copy, scale=0.75)
+
+        h = [sb("h%d" % t, [P, S], F32) for t in range(PACK)]
+        h_acc = []
+        for first, count in Z_CHUNKS:
+            cols = slice(first, first + count)
+            left = sb("left%d" % first, [P, PACK, count], F32)
+            right = sb("right%d" % first, [P, PACK, count], F32)
+            for t in range(PACK):
+                nc.vector.tensor_tensor(
+                    left[:, t, :], d[t][:].indirect(entries(list_tiles["n2"], first, count)), y[t][:, cols], ALU.mult
+                )
+                nc.vector.tensor_tensor(
+                    right[:, t, :], y[t][:].indirect(entries(list_tiles["n1"], first, count)), d[t][:, cols], ALU.mult
+                )
+            z = sb("z%d" % first, [P, count, PACK], BF16)
+            nc.vector.tensor_tensor(as_words(z[:]), by_words(left[:]), by_words(right[:]), ALU.subtract)
+            z_codes = sb("z_codes%d" % first, [P, count], U32)
+            z_plane = sb("z_plane%d" % first, [P, count], U8)
+            nc.vector.quantize_mx(
+                out=z_codes[:].bitcast(FP8X4), scales=z_plane[:], in_=z[:].rearrange("p j t -> p (j t)")
+            )
+            for start in range(0, count, PIECE):
+                c = (first + start) // PIECE
+                acc = psum.tile([P, PACK, PIECE], F32, name="bank%d" % c)
+                h_acc.append(acc)
+                piece = slice(start, start + PIECE)
+                for t in range(PACK):
+                    product(acc[:, t, :], 2, t, z_codes[:, piece], z_plane[:, piece])
+                for t in range(PACK):
+                    nc.scalar.copy(h[t][:, c * PIECE : (c + 1) * PIECE], acc[:, t, :])
+
+        out_rows = out_0.rearrange("(p t) j -> p t j", t=PACK)
+        out_words = out_1[0].rearrange("p c r -> p (c r)").bitcast(I32)
+        o_codes = sb("o_codes", [P, S], U32)
+        o_plane = sb("o_plane", [P, S], U8)
+        for first, count in OUT_CHUNKS:
+            cols = slice(first, first + count)
+            last = first + count == S
+            low = sb("low%d" % first, [P, PACK, count], F32)
+            diff = sb("diff%d" % first, [P, PACK, count], F32)
+            gate = sb("gate%d" % first, [P, PACK, count], F32)
+            for t0 in range(0, PACK, 2):
+                for t in (t0, t0 + 1):
+                    nc.vector.tensor_copy(low[:, t, :], h[t][:].indirect(entries(list_tiles["n4"], first, count)))
+                for t in (t0, t0 + 1):
+                    nc.vector.tensor_tensor(
+                        diff[:, t, :], h[t][:].indirect(entries(list_tiles["n3"], first, count)), low[:, t, :],
+                        ALU.subtract,
+                    )
+                    nc.scalar.activation(gate[:, t, :], diff[:, t, :], ACT.Sigmoid)
+            result = sb("result%d" % first, [P, PACK, count], F32)
+            for start in range(0, count, PIECE):
+                piece = slice(start, start + PIECE)
+                nc.vector.tensor_tensor(
+                    result[:, :, piece], h_acc[(first + start) // PIECE][:], gate[:, :, piece], ALU.mult
+                )
+            nc.sync.dma_start(out=out_rows[:, :, cols], in_=result[:])
+            rounded = sb("rounded%d" % first, [P, count, PACK], BF16)
+            if last:
+                nc.vector.tensor_copy(as_words(rounded[:]), by_words(result[:]))
+            else:
+                nc.scalar.copy(as_words(rounded[:]), by_words(result[:]))
+            nc.vector.quantize_mx(
+                out=o_codes[:, cols].bitcast(FP8X4), scales=o_plane[:, cols],
+                in_=rounded[:].rearrange("p j t -> p (j t)"),
+            )
+            nc.sync.dma_start(out=out_words[:, cols], in_=o_codes[:, cols].bitcast(I32))
+        for q in range(QUADS):
+            queue = nc.scalar if q % 2 == 0 else nc.sync
+            queue.dma_start(
+                out=out_2[0, 4 * q : 4 * q + 4, :].bitcast(I32), in_=o_plane[32 * q : 32 * q + 4, :].bitcast(I32)
+            )

@@ -80,9 +80,11 @@ def tile_picked_twlcrossbcmp_none_po_kernel(
         gain = sb("gain", [P, PACK], F32)
         warm = sb("warm", [P, 2], F32)
 
-        nc.vector.memset(x_plane[:].bitcast(I32), 0)
+        x_plane_words = x_plane[:].bitcast(I32)
+        nc.vector.memset(x_plane_words[:, : T // 8], 0)
+        nc.gpsimd.memset(x_plane_words[:, T // 8 :], 0)
         for i in range(3):
-            nc.gpsimd.memset(w_plane[i][:].bitcast(I32), 0)
+            nc.vector.memset(w_plane[i][:].bitcast(I32), 0)
         nc.vector.memset(warm[:, 0:1], 0.0)
         nc.scalar.activation(warm[:, 1:2], warm[:, 0:1], ACT.Sigmoid)
 
@@ -90,13 +92,13 @@ def tile_picked_twlcrossbcmp_none_po_kernel(
         nc.sync.dma_start(list_tiles["offs"][:], offs)
         nc.sync.dma_start(list_tiles["two"][:], two)
         nc.sync.dma_start(out=w_words[0][:].bitcast(I32), in_=w1_words[0].bitcast(I32))
-        nc.sync.dma_start(out=w_words[1][:].bitcast(I32), in_=w2_words[0].bitcast(I32))
         nc.sync.dma_start(out=x_codes[:].bitcast(I32), in_=x_words[0].rearrange("p n t -> p (n t)").bitcast(I32))
         load_scale_rows(nc.sync, w_plane[0], w1_scales)
+        nc.sync.dma_start(out=w_words[1][:].bitcast(I32), in_=w2_words[0].bitcast(I32))
         load_scale_rows(nc.sync, w_plane[1], w2_scales)
         nc.sync.dma_start(out=gain[:], in_=gn.rearrange("(p t) o -> p (t o)", t=PACK))
-        nc.sync.dma_start(list_tiles["n2"][:], n2)
         nc.sync.dma_start(list_tiles["n1"][:], n1)
+        nc.sync.dma_start(list_tiles["n2"][:], n2)
         nc.sync.dma_start(out=w_words[2][:].bitcast(I32), in_=w3_words[0].bitcast(I32))
         load_scale_rows(nc.sync, w_plane[2], w3_scales)
         nc.sync.dma_start(list_tiles["n4"][:], n4)
@@ -106,20 +108,19 @@ def tile_picked_twlcrossbcmp_none_po_kernel(
         a_plane = sb("a_plane", [P, S], U8)
         b_codes = sb("b_codes", [P, S], U32)
         b_plane = sb("b_plane", [P, S], U8)
+        deal_words(nc.vector, w_words[0], wd_words[0])
         nc.vector.tensor_copy(a_plane[:], x_plane[:].indirect(list_tiles["offs"][:]))
         nc.vector.tensor_copy(b_plane[:], x_plane[:].indirect(list_tiles["two"][:]))
-        deal_words(nc.vector, w_words[0], wd_words[0])
-        deal_words(nc.vector, w_words[1], wd_words[1])
-        deal_plane(nc.vector, w_plane[0], wd_plane[0])
         nc.vector.tensor_copy(a_codes[:], x_codes[:].indirect(list_tiles["offs"][:]))
-        deal_plane(nc.vector, w_plane[1], wd_plane[1])
         half = S // 2
         for first in (0, half):
             nc.vector.tensor_copy(
                 b_codes[:, first : first + half], x_codes[:].indirect(entries(list_tiles["two"], first, half))
             )
-        deal_words(nc.vector, w_words[2], wd_words[2])
-        deal_plane(nc.vector, w_plane[2], wd_plane[2])
+        deal_plane(nc.gpsimd, w_plane[0], wd_plane[0])
+        for i in (1, 2):
+            deal_words(nc.gpsimd, w_words[i], wd_words[i])
+            deal_plane(nc.gpsimd, w_plane[i], wd_plane[i])
 
         def product(acc, w, t, codes, plane):
             nc.tensor.matmul_mx(
@@ -129,18 +130,26 @@ def tile_picked_twlcrossbcmp_none_po_kernel(
 
         y = [sb("y%d" % t, [P, S], F32) for t in range(PACK)]
         d = [sb("d%d" % t, [P, S], F32) for t in range(PACK)]
-        y_acc = [psum.tile([P, S], F32, name="bank%d" % t) for t in range(PACK)]
-        d_acc = [psum.tile([P, S], F32, name="bank%d" % (PACK + t)) for t in range(PACK)]
-        for t in range(PACK):
-            product(y_acc[t][:], 0, t, a_codes[:], a_plane[:])
-        for first in (0, half):
-            cols = slice(first, first + half)
-            product(d_acc[0][:, cols], 1, 0, b_codes[:, cols], b_plane[:, cols])
-        for t in range(1, PACK):
-            product(d_acc[t][:], 1, t, b_codes[:], b_plane[:])
-        for t in range(PACK):
-            nc.scalar.activation(y[t][:], y_acc[t][:], ACT.Copy, scale=gain[:, t : t + 1])
-            nc.scalar.activation(d[t][:], d_acc[t][:], ACT.Copy, scale=0.75)
+        def make_y(t, bank):
+            acc = psum.tile([P, S], F32, name="bank%d" % bank)
+            product(acc[:], 0, t, a_codes[:], a_plane[:])
+            nc.scalar.activation(y[t][:], acc[:], ACT.Copy, scale=gain[:, t : t + 1])
+
+        def make_d(t, bank, width):
+            acc = psum.tile([P, S], F32, name="bank%d" % bank)
+            for first in range(0, S, width):
+                cols = slice(first, first + width)
+                product(acc[:, cols], 1, t, b_codes[:, cols], b_plane[:, cols])
+            nc.scalar.activation(d[t][:], acc[:], ACT.Copy, scale=0.75)
+
+        make_y(0, 0)
+        make_y(1, 1)
+        make_d(0, 4, half)
+        make_d(1, 5, S)
+        make_y(2, 4)
+        make_d(2, 6, S)
+        make_y(3, 5)
+        make_d(3, 7, S)
 
         h = [sb("h%d" % t, [P, S], F32) for t in range(PACK)]
         h_acc = []
@@ -148,13 +157,17 @@ def tile_picked_twlcrossbcmp_none_po_kernel(
             cols = slice(first, first + count)
             left = sb("left%d" % first, [P, PACK, count], F32)
             right = sb("right%d" % first, [P, PACK, count], F32)
+            early = 2 if first == 0 else 0
+            if early:
+                picked = sb("picked", [P, early, count], F32)
+                for t in range(early):
+                    nc.vector.tensor_copy(picked[:, t, :], y[t][:].indirect(entries(list_tiles["n1"], first, count)))
             for t in range(PACK):
                 nc.vector.tensor_tensor(
                     left[:, t, :], d[t][:].indirect(entries(list_tiles["n2"], first, count)), y[t][:, cols], ALU.mult
                 )
-                nc.vector.tensor_tensor(
-                    right[:, t, :], y[t][:].indirect(entries(list_tiles["n1"], first, count)), d[t][:, cols], ALU.mult
-                )
+                y_at = picked[:, t, :] if t < early else y[t][:].indirect(entries(list_tiles["n1"], first, count))
+                nc.vector.tensor_tensor(right[:, t, :], y_at, d[t][:, cols], ALU.mult)
             z = sb("z%d" % first, [P, count, PACK], BF16)
             nc.vector.tensor_tensor(as_words(z[:]), by_words(left[:]), by_words(right[:]), ALU.subtract)
             z_codes = sb("z_codes%d" % first, [P, count], U32)
@@ -182,10 +195,11 @@ def tile_picked_twlcrossbcmp_none_po_kernel(
             low = sb("low%d" % first, [P, PACK, count], F32)
             diff = sb("diff%d" % first, [P, PACK, count], F32)
             gate = sb("gate%d" % first, [P, PACK, count], F32)
-            for t0 in range(0, PACK, 2):
-                for t in (t0, t0 + 1):
+            group = PACK if last else 2
+            for t0 in range(0, PACK, group):
+                for t in range(t0, t0 + group):
                     nc.vector.tensor_copy(low[:, t, :], h[t][:].indirect(entries(list_tiles["n4"], first, count)))
-                for t in (t0, t0 + 1):
+                for t in range(t0, t0 + group):
                     nc.vector.tensor_tensor(
                         diff[:, t, :], h[t][:].indirect(entries(list_tiles["n3"], first, count)), low[:, t, :],
                         ALU.subtract,
@@ -194,9 +208,12 @@ def tile_picked_twlcrossbcmp_none_po_kernel(
             result = sb("result%d" % first, [P, PACK, count], F32)
             for start in range(0, count, PIECE):
                 piece = slice(start, start + PIECE)
-                nc.vector.tensor_tensor(
-                    result[:, :, piece], h_acc[(first + start) // PIECE][:], gate[:, :, piece], ALU.mult
-                )
+                rows = 1 if last else PACK
+                for t0 in range(0, PACK, rows):
+                    ts = slice(t0, t0 + rows)
+                    nc.vector.tensor_tensor(
+                        result[:, ts, piece], h_acc[(first + start) // PIECE][:, ts, :], gate[:, ts, piece], ALU.mult
+                    )
             nc.sync.dma_start(out=out_rows[:, :, cols], in_=result[:])
             rounded = sb("rounded%d" % first, [P, count, PACK], BF16)
             if last:

from contextlib import ExitStack

import concourse.mybir as mybir

K, T, S, N, H = 512, 2048, 512, 512, 512
FLOPS = 3 * 2 * 512 * 512 * 512

F32 = mybir.dt.float32
BF16 = mybir.dt.bfloat16
I32 = mybir.dt.int32
U32 = mybir.dt.uint32
U16 = mybir.dt.uint16
U8 = mybir.dt.uint8
FP8X4 = mybir.dt.float8_e4m3fn_x4
FP4X4 = mybir.dt.float4_e2m1fn_x4
ALU = mybir.AluOpType
ACT = mybir.ActivationFunctionType

P = 128
PACK = 4
QUADS = 4
LIST_ROWS = 16
PIECE = 128
Z_CHUNKS = ((0, 256), (256, 128), (384, 128))
OUT_CHUNKS = ((0, 256), (256, 128), (384, 128))


def entries(lst, first, count):
    return lst[:, first // LIST_ROWS : (first + count) // LIST_ROWS]


def load_scale_rows(queue, plane, scales):
    rows = scales[0].bitcast(I32).rearrange("(q r) c -> r q c", r=4)
    for r in range(4):
        queue.dma_start(out=plane[r:P:32, :].bitcast(I32), in_=rows[r])


def deal_words(engine, words, dealt):
    engine.tensor_copy(
        out=dealt[:].rearrange("p t (m e) -> p t m e", e=2),
        in_=words[:].rearrange("p (m t e) -> p t m e", t=PACK, e=2),
    )


def deal_plane(engine, plane, dealt):
    engine.tensor_copy(out=dealt[:], in_=plane[:].rearrange("p (m t) -> p t m", t=PACK))


def by_words(tile_pt):
    return tile_pt.rearrange("p t (c i) -> p c t i", i=4)


def as_words(tile_words):
    return tile_words.rearrange("p (c i) t -> p c t i", i=4)


def tile_picked_twlcrossbcmp_none_po_kernel(
    tc, x_words, x_scales, w1_words, w1_scales, w2_words, w2_scales, gn, w3_words, w3_scales,
    offs, two, n1, n2, n3, n4, out_0, out_1, out_2,
):
    nc = tc.nc
    with ExitStack() as ctx:
        lists = ctx.enter_context(tc.tile_pool(name="lists", bufs=1))
        keep = ctx.enter_context(tc.tile_pool(name="keep", bufs=1))
        psum = ctx.enter_context(tc.psum_pool(name="psum", bufs=1))

        def sb(name, shape, dtype):
            return keep.tile(shape, dtype, name=name, align_bytes=64)

        list_tiles = {}
        for name in ("offs", "two", "n1", "n2", "n3", "n4"):
            list_tiles[name] = lists.tile([P, S // LIST_ROWS], U16, name=name)

        x_plane = sb("x_plane", [P, T], U8)
        x_codes = sb("x_codes", [P, T], U32)
        w_words = [sb("w_words%d" % i, [P, 2 * H], U8) for i in range(3)]
        w_plane = [sb("w_plane%d" % i, [P, H], U8) for i in range(3)]
        wd_words = [sb("wd_words%d" % i, [P, PACK, 2 * P], U8) for i in range(3)]
        wd_plane = [sb("wd_plane%d" % i, [P, PACK, P], U8) for i in range(3)]
        gain = sb("gain", [P, PACK], F32)
        warm = sb("warm", [P, 2], F32)

        x_plane_words = x_plane[:].bitcast(I32)
        nc.vector.memset(x_plane_words[:, : T // 8], 0)
        nc.gpsimd.memset(x_plane_words[:, T // 8 :], 0)
        for i in range(3):
            nc.vector.memset(w_plane[i][:].bitcast(I32), 0)
        nc.vector.memset(warm[:, 0:1], 0.0)
        nc.scalar.activation(warm[:, 1:2], warm[:, 0:1], ACT.Sigmoid)

        load_scale_rows(nc.sync, x_plane, x_scales)
        nc.sync.dma_start(list_tiles["offs"][:], offs)
        nc.sync.dma_start(list_tiles["two"][:], two)
        nc.sync.dma_start(out=w_words[0][:].bitcast(I32), in_=w1_words[0].bitcast(I32))
        nc.sync.dma_start(out=x_codes[:].bitcast(I32), in_=x_words[0].rearrange("p n t -> p (n t)").bitcast(I32))
        load_scale_rows(nc.sync, w_plane[0], w1_scales)
        nc.sync.dma_start(out=w_words[1][:].bitcast(I32), in_=w2_words[0].bitcast(I32))
        load_scale_rows(nc.sync, w_plane[1], w2_scales)
        nc.sync.dma_start(out=gain[:], in_=gn.rearrange("(p t) o -> p (t o)", t=PACK))
        nc.sync.dma_start(list_tiles["n1"][:], n1)
        nc.sync.dma_start(list_tiles["n2"][:], n2)
        nc.sync.dma_start(out=w_words[2][:].bitcast(I32), in_=w3_words[0].bitcast(I32))
        load_scale_rows(nc.sync, w_plane[2], w3_scales)
        nc.sync.dma_start(list_tiles["n4"][:], n4)
        nc.sync.dma_start(list_tiles["n3"][:], n3)

        a_codes = sb("a_codes", [P, S], U32)
        a_plane = sb("a_plane", [P, S], U8)
        b_codes = sb("b_codes", [P, S], U32)
        b_plane = sb("b_plane", [P, S], U8)
        deal_words(nc.vector, w_words[0], wd_words[0])
        nc.vector.tensor_copy(a_plane[:], x_plane[:].indirect(list_tiles["offs"][:]))
        nc.vector.tensor_copy(b_plane[:], x_plane[:].indirect(list_tiles["two"][:]))
        nc.vector.tensor_copy(a_codes[:], x_codes[:].indirect(list_tiles["offs"][:]))
        half = S // 2
        for first in (0, half):
            nc.vector.tensor_copy(
                b_codes[:, first : first + half], x_codes[:].indirect(entries(list_tiles["two"], first, half))
            )
        deal_plane(nc.gpsimd, w_plane[0], wd_plane[0])
        for i in (1, 2):
            deal_words(nc.gpsimd, w_words[i], wd_words[i])
            deal_plane(nc.gpsimd, w_plane[i], wd_plane[i])

        def product(acc, w, t, codes, plane):
            nc.tensor.matmul_mx(
                out=acc, lhsT=wd_words[w][:, t, :].bitcast(FP4X4), lhsT_scale=wd_plane[w][:, t, :],
                rhs=codes.bitcast(FP8X4), rhs_scale=plane, start=True, stop=True,
            )

        y = [sb("y%d" % t, [P, S], F32) for t in range(PACK)]
        d = [sb("d%d" % t, [P, S], F32) for t in range(PACK)]
        def make_y(t, bank):
            acc = psum.tile([P, S], F32, name="bank%d" % bank)
            product(acc[:], 0, t, a_codes[:], a_plane[:])
            nc.scalar.activation(y[t][:], acc[:], ACT.Copy, scale=gain[:, t : t + 1])

        def make_d(t, bank, width):
            acc = psum.tile([P, S], F32, name="bank%d" % bank)
            for first in range(0, S, width):
                cols = slice(first, first + width)
                product(acc[:, cols], 1, t, b_codes[:, cols], b_plane[:, cols])
            nc.scalar.activation(d[t][:], acc[:], ACT.Copy, scale=0.75)

        make_y(0, 0)
        make_y(1, 1)
        make_d(0, 4, half)
        make_d(1, 5, S)
        make_y(2, 4)
        make_d(2, 6, S)
        make_y(3, 5)
        make_d(3, 7, S)

        h = [sb("h%d" % t, [P, S], F32) for t in range(PACK)]
        h_acc = []
        for first, count in Z_CHUNKS:
            cols = slice(first, first + count)
            left = sb("left%d" % first, [P, PACK, count], F32)
            right = sb("right%d" % first, [P, PACK, count], F32)
            early = 2 if first == 0 else 0
            if early:
                picked = sb("picked", [P, early, count], F32)
                for t in range(early):
                    nc.vector.tensor_copy(picked[:, t, :], y[t][:].indirect(entries(list_tiles["n1"], first, count)))
            for t in range(PACK):
                nc.vector.tensor_tensor(
                    left[:, t, :], d[t][:].indirect(entries(list_tiles["n2"], first, count)), y[t][:, cols], ALU.mult
                )
                y_at = picked[:, t, :] if t < early else y[t][:].indirect(entries(list_tiles["n1"], first, count))
                nc.vector.tensor_tensor(right[:, t, :], y_at, d[t][:, cols], ALU.mult)
            z = sb("z%d" % first, [P, count, PACK], BF16)
            nc.vector.tensor_tensor(as_words(z[:]), by_words(left[:]), by_words(right[:]), ALU.subtract)
            z_codes = sb("z_codes%d" % first, [P, count], U32)
            z_plane = sb("z_plane%d" % first, [P, count], U8)
            nc.vector.quantize_mx(
                out=z_codes[:].bitcast(FP8X4), scales=z_plane[:], in_=z[:].rearrange("p j t -> p (j t)")
            )
            for start in range(0, count, PIECE):
                c = (first + start) // PIECE
                acc = psum.tile([P, PACK, PIECE], F32, name="bank%d" % c)
                h_acc.append(acc)
                piece = slice(start, start + PIECE)
                for t in range(PACK):
                    product(acc[:, t, :], 2, t, z_codes[:, piece], z_plane[:, piece])
                for t in range(PACK):
                    nc.scalar.copy(h[t][:, c * PIECE : (c + 1) * PIECE], acc[:, t, :])

        out_rows = out_0.rearrange("(p t) j -> p t j", t=PACK)
        out_words = out_1[0].rearrange("p c r -> p (c r)").bitcast(I32)
        o_codes = sb("o_codes", [P, S], U32)
        o_plane = sb("o_plane", [P, S], U8)
        for first, count in OUT_CHUNKS:
            cols = slice(first, first + count)
            last = first + count == S
            low = sb("low%d" % first, [P, PACK, count], F32)
            diff = sb("diff%d" % first, [P, PACK, count], F32)
            gate = sb("gate%d" % first, [P, PACK, count], F32)
            group = PACK if last else 2
            for t0 in range(0, PACK, group):
                for t in range(t0, t0 + group):
                    nc.vector.tensor_copy(low[:, t, :], h[t][:].indirect(entries(list_tiles["n4"], first, count)))
                for t in range(t0, t0 + group):
                    nc.vector.tensor_tensor(
                        diff[:, t, :], h[t][:].indirect(entries(list_tiles["n3"], first, count)), low[:, t, :],
                        ALU.subtract,
                    )
                    nc.scalar.activation(gate[:, t, :], diff[:, t, :], ACT.Sigmoid)
            result = sb("result%d" % first, [P, PACK, count], F32)
            for start in range(0, count, PIECE):
                piece = slice(start, start + PIECE)
                rows = 1 if last else PACK
                for t0 in range(0, PACK, rows):
                    ts = slice(t0, t0 + rows)
                    nc.vector.tensor_tensor(
                        result[:, ts, piece], h_acc[(first + start) // PIECE][:, ts, :], gate[:, ts, piece], ALU.mult
                    )
            nc.sync.dma_start(out=out_rows[:, :, cols], in_=result[:])
            rounded = sb("rounded%d" % first, [P, count, PACK], BF16)
            if last:
                nc.vector.tensor_copy(as_words(rounded[:]), by_words(result[:]))
            else:
                nc.scalar.copy(as_words(rounded[:]), by_words(result[:]))
            nc.vector.quantize_mx(
                out=o_codes[:, cols].bitcast(FP8X4), scales=o_plane[:, cols],
                in_=rounded[:].rearrange("p j t -> p (j t)"),
            )
            nc.sync.dma_start(out=out_words[:, cols], in_=o_codes[:, cols].bitcast(I32))
        for q in range(QUADS):
            queue = nc.scalar if q % 2 == 0 else nc.sync
            queue.dma_start(
                out=out_2[0, 4 * q : 4 * q + 4, :].bitcast(I32), in_=o_plane[32 * q : 32 * q + 4, :].bitcast(I32)
            )
